import numpy as np
import ml_dtypes


def mxq(x, axis, fmt="e4m3"):
    dtype, down = {"e4m3": (ml_dtypes.float8_e4m3fn, 7), "e5m2": (ml_dtypes.float8_e5m2, 14)}[fmt]
    v = np.moveaxis(np.asarray(x, np.float32).astype(ml_dtypes.bfloat16).astype(np.float64), axis, -1)
    blocks = v.reshape(v.shape[:-1] + (-1, 32))
    amax = np.abs(blocks).max(-1, keepdims=True)
    byte = np.maximum(np.where(amax > 0, np.frexp(amax)[1] - 1 + 127, 0) - down, 1)
    scale = np.exp2(byte - 127.0)
    codes = (blocks / scale).astype(np.float32).astype(dtype).astype(np.float64)
    return np.moveaxis((codes * scale).reshape(v.shape), -1, axis)


WIDE = False


def mx_kscale(k):
    if not WIDE:
        return np.ones(k)
    levels = np.array([10, -10, 5, -5, 0])
    if k % 512:
        return np.exp2(np.random.permutation(np.resize(levels, k // 32))).repeat(32)
    a = np.empty((k // 512, 16))
    for p in range(k // 512):
        a[p, :8] = np.random.permutation(np.resize(levels, 8))
        for g in range(8):
            far = levels[np.abs(levels - a[p, g]) >= 10]
            a[p, g + 8] = far[np.random.randint(len(far))]
    return np.exp2(a.ravel()).repeat(32)


def f64(x):
    return np.asarray(x).astype(np.float64)


def striped(idx):
    return np.tile(idx.reshape(-1, 16).T, (8, 1)).astype(np.uint16)


def unstriped(offs):
    return offs[:16].T.reshape(-1).astype(np.int64)


def striped8(idx):
    return np.concatenate([x.reshape(-1, 16).T for x in idx]).astype(np.uint16)


def runs(offs, k):
    lists = np.stack([offs[16 * r : 16 * r + 16].T.reshape(-1) for r in range(8)]).astype(np.int64)
    return lists[np.arange(k) % 512 // 64]


def pack_weight(w):
    k, n = w.shape
    w = f64(np.asarray(w, np.float32).astype(ml_dtypes.bfloat16)).reshape(k // 32, 32, n)
    amax = np.abs(w).max(1)
    byte = np.clip(np.where(amax > 0, np.frexp(amax)[1] - 1 + 127 - 7, 1), 1, 254)
    scaled = (w * np.exp2(127.0 - byte)[:, None, :]).reshape(k, n).astype(np.float32)
    words = np.ascontiguousarray(scaled.reshape(k // 512, 128, 4, n).transpose(0, 1, 3, 2)).astype(ml_dtypes.float8_e4m3fn).view(np.uint8)
    return words, np.ascontiguousarray(byte.astype(np.uint8).reshape(k // 512, 16, n))


def unpack_weight(words, scales):
    g, p, n, _ = words.shape
    vals = np.ascontiguousarray(words).view(ml_dtypes.float8_e4m3fn).astype(np.float64) * np.repeat(np.exp2(scales.astype(np.float64) - 127.0), 8, axis=1)[..., None]
    return vals.transpose(0, 1, 3, 2).reshape(g * 512, n)


E2M1 = np.array([0.0, 0.5, 1.0, 1.5, 2.0, 3.0, 4.0, 6.0, -0.0, -0.5, -1.0, -1.5, -2.0, -3.0, -4.0, -6.0])


def pack_fp4(w):
    k, n = w.shape
    w = f64(np.asarray(w, np.float32).astype(ml_dtypes.bfloat16)).reshape(k // 32, 32, n)
    amax = np.abs(w).max(1)
    mant, ex = np.frexp(amax / 6.0)
    byte = np.clip(np.where(amax > 0, np.where(mant > 0.5, ex, ex - 1) + 127, 1), 1, 254)
    scaled = (w * np.exp2(127.0 - byte)[:, None, :]).reshape(k, n).astype(np.float32)
    c = np.ascontiguousarray(scaled.reshape(k // 512, 128, 4, n).transpose(0, 1, 3, 2)).astype(ml_dtypes.float4_e2m1fn).view(np.uint8) & 0xF
    words = (c[..., 0::2] | (c[..., 1::2] << 4)).reshape(k // 512, 128, 2 * n)
    return np.ascontiguousarray(words), np.ascontiguousarray(byte.astype(np.uint8).reshape(k // 512, 16, n))


def unpack_fp4(words, scales):
    g, _, n = scales.shape
    words = np.ascontiguousarray(words).reshape(g, 128, n, 2)
    nib = np.empty((g, 128, n, 4), np.uint8)
    nib[..., 0::2] = words & 0xF
    nib[..., 1::2] = words >> 4
    vals = E2M1[nib] * np.repeat(np.exp2(scales.astype(np.float64) - 127.0), 8, axis=1)[..., None]
    return vals.transpose(0, 1, 3, 2).reshape(g * 512, n)


def planes(y):
    n, m = y.shape
    v = y.astype(np.float32).astype(ml_dtypes.bfloat16).astype(np.float64).reshape(n // 32, 32, m)
    top = np.abs(v).max(1)
    byte = np.clip(np.where(top > 0, np.frexp(top)[1] - 1 + 127 - 7, 1), 1, 254)
    codes = (v * np.exp2(127.0 - byte)[:, None, :]).reshape(n, m).astype(np.float32).astype(ml_dtypes.float8_e4m3fn).view(np.uint8)
    words = codes.reshape(n // 512, 128, 4, m).transpose(0, 1, 3, 2)
    return np.ascontiguousarray(words), np.ascontiguousarray(byte.astype(np.uint8).reshape(n // 512, 16, m))


K, T, S, H, C = 512, 2048, 512, 512, 512


def setup_inputs():
    n = np.random.standard_normal
    s = mx_kscale(K)[:, None]
    packed_xT = pack_weight(n((K, T)) * s)
    packed_w1 = pack_fp4(n((K, H)) / np.sqrt(K) / s)
    return {
        "x_words": packed_xT[0],
        "x_scales": packed_xT[1],
        "w1_words": packed_w1[0],
        "w1_scales": packed_w1[1],
        "gs": (np.random.uniform(0.5, 1.5, (K, 1)) / s).astype(np.float32),
        "offs": striped(np.random.permutation(T)[:S]),
        "n1": striped(np.random.permutation(S)),
        "n2": striped(np.random.permutation(S)),
        "ca": striped(np.random.permutation(T)[:C]),
        "cb": striped(np.random.permutation(T)[:C]),
        "n3": striped8(np.stack([np.random.permutation(S) for _ in range(8)])),
        "n4": striped8(np.stack([np.random.permutation(S) for _ in range(8)])),
    }


def reference(x_words, x_scales, w1_words, w1_scales, gs, offs, n1, n2, ca, cb, n3, n4):
    x_ca = unpack_weight(x_words, x_scales)[:, unstriped(ca)]
    xq = unpack_weight(x_words, x_scales)[:, unstriped(offs)]
    y = unpack_fp4(w1_words, w1_scales).T @ xq
    z = f64(gs) * (y[:, unstriped(n1)] / (np.abs(y) + np.abs(y[:, unstriped(n2)]) + 0.5))
    zq = mxq(z, 0, "e4m3")
    a = 0.0625 * (x_ca.T @ zq)
    x_cb = unpack_weight(x_words, x_scales)[:, unstriped(cb)]
    b = 0.0625 * (x_cb.T @ zq)
    out_0 = a[np.arange(C)[:, None], runs(n3, C)] - (np.tanh(b) * (b[np.arange(C)[:, None], runs(n4, C)]))
    return (out_0,) + planes(out_0)

@@ -1,0 +1,204 @@
+from contextlib import ExitStack
+
+import concourse.mybir as mybir
+
+F32 = mybir.dt.float32
+BF16 = mybir.dt.bfloat16
+I32 = mybir.dt.int32
+U32 = mybir.dt.uint32
+U16 = mybir.dt.uint16
+U8 = mybir.dt.uint8
+FP8X4 = mybir.dt.float8_e4m3fn_x4
+FP4X4 = mybir.dt.float4_e2m1fn_x4
+ACT = mybir.ActivationFunctionType
+ALU = mybir.AluOpType
+
+P = 128
+PACK = 4
+T = 2048
+S = 512
+PER_COL = 16
+SPARE = 32
+RUN = 4
+Z_CHUNKS = ((0, 256), (256, 512))
+OUT_CHUNKS = ((0, 256), (256, 384), (384, 512))
+SIXTEENTH = 0.0625
+
+FLOPS = 3 * 2 * 512 * 512 * 512
+
+
+def list_slice(offsets, c0, c1):
+    return offsets[:, c0 // PER_COL : c1 // PER_COL]
+
+
+def tile_picked_ccmpsoftbnorm2_none_po_kernel(
+    tc, x_words, x_scales, w1_words, w1_scales, gs, offs, n1, n2, ca, cb, n3, n4, out_0, out_1, out_2
+):
+    nc = tc.nc
+    with ExitStack() as ctx:
+        lists = ctx.enter_context(tc.tile_pool(name="lists", bufs=1))
+        sb = ctx.enter_context(tc.tile_pool(name="sb", bufs=1))
+        psum = ctx.enter_context(tc.psum_pool(name="psum", bufs=1))
+
+        def load_list(name, src):
+            tile = lists.tile([P, S // PER_COL], U16, name=name)
+            nc.sync.dma_start(tile[:], src)
+            return tile
+
+        x_sc = sb.tile([P, T], U8, name="x_sc", align_bytes=64)
+        w_sc_raw = sb.tile([P, S], U8, name="w_sc_raw", tag="w_sc_raw", align_bytes=64)
+        nc.vector.memset(x_sc[:].bitcast(I32), 0)
+        nc.gpsimd.memset(w_sc_raw[:].bitcast(I32), 0)
+        x_w = sb.tile([P, T], U32, name="x_w", align_bytes=64)
+        w_raw = sb.tile([P, 2 * S], U8, name="w_raw", align_bytes=64)
+        offs_l = load_list("offs_l", offs)
+        nc.sync.dma_start(w_raw[:].bitcast(I32), w1_words[0].bitcast(I32))
+        nc.sync.dma_start(x_w[:].bitcast(I32), x_words[0].rearrange("p n t -> p (n t)").bitcast(I32))
+        for q in range(4):
+            nc.scalar.dma_start(x_sc[32 * q : 32 * q + 4, :].bitcast(I32), x_scales[0, 4 * q : 4 * q + 4, :].bitcast(I32))
+        for q in range(4):
+            queue = nc.gpsimd if q >= 2 else nc.scalar
+            queue.dma_start(w_sc_raw[32 * q : 32 * q + 4, :].bitcast(I32), w1_scales[0, 4 * q : 4 * q + 4, :].bitcast(I32))
+        cb_l = load_list("cb_l", cb)
+        ca_l = load_list("ca_l", ca)
+        n2_l = load_list("n2_l", n2)
+        gs_sb = sb.tile([P, PACK], F32, name="gs_sb")
+        nc.sync.dma_start(gs_sb[:], gs.rearrange("(p t) o -> p (t o)", t=PACK))
+        n1_l = load_list("n1_l", n1)
+        n4_l = load_list("n4_l", n4)
+        n3_l = load_list("n3_l", n3)
+
+        y_abs = [sb.tile([P, S + SPARE], F32, name=f"y_abs{t}") for t in range(PACK)]
+        for t in range(PACK):
+            nc.gpsimd.memset(y_abs[t][:, S:], 0.0)
+
+        w_codes = sb.tile([P, 2 * S], U8, name="w_codes", align_bytes=64)
+        nc.vector.tensor_copy(
+            w_codes[:].rearrange("p (t m b) -> p t m b", t=PACK, b=2),
+            w_raw[:].rearrange("p (m t b) -> p t m b", t=PACK, b=2),
+        )
+        xq_sc = sb.tile([P, S], U8, name="xq_sc", align_bytes=64)
+        nc.vector.tensor_copy(xq_sc[:], x_sc[:].indirect(offs_l[:]))
+        w_sc = sb.tile([P, S], U8, name="w_sc", align_bytes=64)
+        nc.vector.tensor_copy(
+            w_sc[:].rearrange("p (t m) -> p t m", t=PACK),
+            w_sc_raw[:].rearrange("p (m t) -> p t m", t=PACK),
+        )
+        xq_w = sb.tile([P, S], U32, name="xq_w", align_bytes=64)
+        nc.vector.tensor_copy(xq_w[:], x_w[:].indirect(offs_l[:]))
+
+        y_ps = [psum.tile([P, S], F32, name=f"y_ps{t}", tag=f"bank{t}") for t in range(PACK)]
+        for t in range(PACK):
+            nc.tensor.matmul_mx(
+                y_ps[t][:],
+                lhsT=w_codes[:, 2 * P * t : 2 * P * (t + 1)].bitcast(FP4X4),
+                lhsT_scale=w_sc[:, P * t : P * (t + 1)],
+                rhs=xq_w[:].bitcast(FP8X4),
+                rhs_scale=xq_sc[:],
+                start=True,
+                stop=True,
+            )
+
+        pair_w_raw = sb.tile([P, 2, S], U32, name="pair_w_raw", align_bytes=64)
+        pair_sc_raw = sb.tile([P, 2, S], U8, name="pair_sc_raw", tag="w_sc_raw", align_bytes=64)
+        pair_w = sb.tile([P, 2, S], U32, name="pair_w", align_bytes=64)
+        pair_sc = sb.tile([P, 2, S], U8, name="pair_sc", align_bytes=64)
+        for side, offsets in enumerate((cb_l, ca_l)):
+            nc.vector.tensor_copy(pair_sc_raw[:, side, :], x_sc[:].indirect(offsets[:]))
+        for side, offsets in enumerate((cb_l, ca_l)):
+            nc.vector.tensor_copy(pair_w_raw[:, side, :], x_w[:].indirect(offsets[:]))
+
+        y_sb = [sb.tile([P, S], F32, name=f"y_sb{t}") for t in range(PACK)]
+        y_n2 = [sb.tile([P, S], F32, name=f"y_n2{t}") for t in range(PACK)]
+        den = [sb.tile([P, S], F32, name=f"den{t}", tag=f"den{t}") for t in range(PACK)]
+        root = [sb.tile([P, S], F32, name=f"root{t}") for t in range(PACK)]
+        factor = sb.tile([P, PACK, S], F32, name="factor")
+        for t in range(PACK):
+            nc.scalar.activation(y_abs[t][:, :S], y_ps[t][:], ACT.Abs)
+            nc.scalar.activation(y_n2[t][:], y_abs[t][:].indirect(n2_l[:]), ACT.Copy)
+        for t in range(PACK):
+            nc.gpsimd.tensor_tensor(den[t][:], y_abs[t][:, :S], y_n2[t][:], ALU.add)
+            nc.vector.tensor_copy(y_sb[t][:], y_ps[t][:])
+        for t in range(PACK):
+            nc.scalar.activation(root[t][:], den[t][:], ACT.Abs_reciprocal_sqrt, bias=0.5)
+        for t in range(PACK):
+            nc.vector.scalar_tensor_tensor(factor[:, t, :], root[t][:], gs_sb[:, t : t + 1], root[t][:], ALU.mult, ALU.mult)
+
+        nc.vector.tensor_copy(
+            pair_w[:].bitcast(I32).rearrange("p s (t m) -> p s t m", t=PACK),
+            pair_w_raw[:].bitcast(I32).rearrange("p s (m t) -> p s t m", t=PACK),
+        )
+        nc.vector.tensor_copy(
+            pair_sc[:].rearrange("p s (t m) -> p s t m", t=PACK),
+            pair_sc_raw[:].rearrange("p s (m t) -> p s t m", t=PACK),
+        )
+
+        b_banks = [psum.tile([P, 2, S // 2], F32, name=f"b_bank{n}", tag=f"bank{PACK + n}") for n in range(PACK)]
+        a_ps = [psum.tile([P, S], F32, name=f"a_ps{t}", tag=f"bank{t}") for t in range(PACK)]
+        b_sb = [sb.tile([P, 2 * S], F32, name=f"b_sb{t}", tag=f"b_sb{t}") for t in range(PACK)]
+        a_sb = [sb.tile([P, S], F32, name=f"a_sb{t}") for t in range(PACK)]
+        y_n1_of = {}
+        for n, (c0, c1) in enumerate(Z_CHUNKS):
+            y_n1_of[c0] = sb.tile([P, PACK, c1 - c0], F32, name=f"y_n1_{c0}", tag=f"den{PACK - 1 - n}")
+            for t in range(PACK):
+                nc.scalar.activation(y_n1_of[c0][:, t, :], y_sb[t][:].indirect(list_slice(n1_l, c0, c1)), ACT.Copy)
+        for n, (c0, c1) in enumerate(Z_CHUNKS):
+            w = c1 - c0
+            y_n1 = y_n1_of[c0]
+            b_ps = [b_banks[2 * n + t // 2][:, t % 2, :] for t in range(PACK)]
+            z_bf = sb.tile([P, w * PACK], BF16, name=f"z_bf{c0}", align_bytes=64)
+            nc.vector.tensor_tensor(
+                z_bf[:].rearrange("p (c i t) -> p c t i", i=RUN, t=PACK),
+                y_n1[:].rearrange("p t (c i) -> p c t i", i=RUN),
+                factor[:, :, c0:c1].rearrange("p t (c i) -> p c t i", i=RUN),
+                ALU.mult,
+            )
+            z_w = sb.tile([P, w], U32, name=f"z_w{c0}", align_bytes=64)
+            z_sc = sb.tile([P, w], U8, name=f"z_sc{c0}", align_bytes=64)
+            nc.vector.quantize_mx(z_w[:].bitcast(FP8X4), z_sc[:], z_bf[:])
+            for side, sums in enumerate((b_ps, [bank[:, c0:c1] for bank in a_ps])):
+                for t in range(PACK):
+                    nc.tensor.matmul_mx(
+                        sums[t],
+                        lhsT=pair_w[:, side, P * t : P * (t + 1)].bitcast(FP8X4),
+                        lhsT_scale=pair_sc[:, side, P * t : P * (t + 1)],
+                        rhs=z_w[:].bitcast(FP8X4),
+                        rhs_scale=z_sc[:],
+                        start=True,
+                        stop=True,
+                    )
+            for t in range(PACK):
+                nc.scalar.activation(b_sb[t][:, S + c0 : S + c1], b_ps[t], ACT.Tanh, scale=SIXTEENTH)
+            for t in range(PACK):
+                nc.vector.tensor_scalar(b_sb[t][:, c0:c1], b_ps[t], SIXTEENTH, None, ALU.mult)
+
+        b_n4 = [sb.tile([P, S], F32, name=f"b_n4{t}", tag=f"b_n4{t}") for t in range(PACK)]
+        prod = sb.tile([P, PACK, S], F32, name="prod")
+        for t in range(PACK):
+            nc.scalar.activation(b_n4[t][:], b_sb[t][:].indirect(n4_l[:]), ACT.Copy)
+        for t in range(PACK):
+            nc.vector.tensor_scalar(a_sb[t][:], a_ps[t][:], SIXTEENTH, None, ALU.mult)
+            nc.vector.tensor_tensor(prod[:, t, :], b_sb[t][:, S:], b_n4[t][:], ALU.mult)
+
+        out_rows = out_0.rearrange("(p t) j -> p t j", t=PACK)
+        out_words = out_1[0].rearrange("p n t -> p (n t)").bitcast(I32)
+        o_sc = sb.tile([P, S], U8, name="o_sc", align_bytes=64)
+        for (c0, c1), freed in zip(OUT_CHUNKS, ("b_sb2", "b_sb3", "b_n43")):
+            w = c1 - c0
+            a_n3 = sb.tile([P, PACK, w], F32, name=f"a_n3_{c0}", tag=freed)
+            for t in range(PACK):
+                nc.scalar.activation(a_n3[:, t, :], a_sb[t][:].indirect(list_slice(n3_l, c0, c1)), ACT.Copy)
+            res = sb.tile([P, PACK, w], F32, name=f"res{c0}")
+            nc.vector.tensor_tensor(res[:], a_n3[:], prod[:, :, c0:c1], ALU.subtract)
+            nc.sync.dma_start(out_rows[:, :, c0:c1], res[:])
+            o_bf = sb.tile([P, w * PACK], BF16, name=f"o_bf{c0}", align_bytes=64)
+            nc.vector.tensor_copy(
+                o_bf[:].rearrange("p (c i t) -> p c t i", i=RUN, t=PACK),
+                res[:].rearrange("p t (c i) -> p c t i", i=RUN),
+            )
+            o_w = sb.tile([P, w], U32, name=f"o_w{c0}", align_bytes=64)
+            nc.vector.quantize_mx(o_w[:].bitcast(FP8X4), o_sc[:, c0:c1], o_bf[:])
+            nc.sync.dma_start(out_words[:, c0:c1], o_w[:].bitcast(I32))
+        for q in range(4):
+            queue = nc.scalar if q % 2 else nc.sync
+            queue.dma_start(out_2[0, 4 * q : 4 * q + 4, :].bitcast(I32), o_sc[32 * q : 32 * q + 4, :].bitcast(I32))

@@ -47,18 +47,17 @@ def tile_picked_ccmpsoftbnorm2_none_po_kernel(
 
         x_sc = sb.tile([P, T], U8, name="x_sc", align_bytes=64)
         w_sc_raw = sb.tile([P, S], U8, name="w_sc_raw", tag="w_sc_raw", align_bytes=64)
-        nc.vector.memset(x_sc[:].bitcast(I32), 0)
+        nc.gpsimd.memset(x_sc[:].bitcast(I32), 0)
         nc.gpsimd.memset(w_sc_raw[:].bitcast(I32), 0)
         x_w = sb.tile([P, T], U32, name="x_w", align_bytes=64)
         w_raw = sb.tile([P, 2 * S], U8, name="w_raw", align_bytes=64)
         offs_l = load_list("offs_l", offs)
         nc.sync.dma_start(w_raw[:].bitcast(I32), w1_words[0].bitcast(I32))
+        for q in range(4):
+            nc.sync.dma_start(x_sc[32 * q : 32 * q + 4, :].bitcast(I32), x_scales[0, 4 * q : 4 * q + 4, :].bitcast(I32))
         nc.sync.dma_start(x_w[:].bitcast(I32), x_words[0].rearrange("p n t -> p (n t)").bitcast(I32))
         for q in range(4):
-            nc.scalar.dma_start(x_sc[32 * q : 32 * q + 4, :].bitcast(I32), x_scales[0, 4 * q : 4 * q + 4, :].bitcast(I32))
-        for q in range(4):
-            queue = nc.gpsimd if q >= 2 else nc.scalar
-            queue.dma_start(w_sc_raw[32 * q : 32 * q + 4, :].bitcast(I32), w1_scales[0, 4 * q : 4 * q + 4, :].bitcast(I32))
+            nc.sync.dma_start(w_sc_raw[32 * q : 32 * q + 4, :].bitcast(I32), w1_scales[0, 4 * q : 4 * q + 4, :].bitcast(I32))
         cb_l = load_list("cb_l", cb)
         ca_l = load_list("ca_l", ca)
         n2_l = load_list("n2_l", n2)
@@ -70,21 +69,23 @@ def tile_picked_ccmpsoftbnorm2_none_po_kernel(
 
         y_abs = [sb.tile([P, S + SPARE], F32, name=f"y_abs{t}") for t in range(PACK)]
         for t in range(PACK):
-            nc.gpsimd.memset(y_abs[t][:, S:], 0.0)
+            nc.vector.memset(y_abs[t][:, S:], 0.0)
+        warm = sb.tile([P, 1], F32, name="warm")
+        nc.scalar.activation(warm[:], y_abs[0][:, S : S + 1], ACT.Abs_reciprocal_sqrt, bias=0.5)
 
-        w_codes = sb.tile([P, 2 * S], U8, name="w_codes", align_bytes=64)
+        w_codes = sb.tile([P, 2 * S], U8, name="w_codes", tag="w_codes", align_bytes=64)
         nc.vector.tensor_copy(
             w_codes[:].rearrange("p (t m b) -> p t m b", t=PACK, b=2),
             w_raw[:].rearrange("p (m t b) -> p t m b", t=PACK, b=2),
         )
-        xq_sc = sb.tile([P, S], U8, name="xq_sc", align_bytes=64)
+        xq_sc = sb.tile([P, S], U8, name="xq_sc", tag="xq_sc", align_bytes=64)
         nc.vector.tensor_copy(xq_sc[:], x_sc[:].indirect(offs_l[:]))
         w_sc = sb.tile([P, S], U8, name="w_sc", align_bytes=64)
         nc.vector.tensor_copy(
             w_sc[:].rearrange("p (t m) -> p t m", t=PACK),
             w_sc_raw[:].rearrange("p (m t) -> p t m", t=PACK),
         )
-        xq_w = sb.tile([P, S], U32, name="xq_w", align_bytes=64)
+        xq_w = sb.tile([P, S], U32, name="xq_w", tag="xq_w", align_bytes=64)
         nc.vector.tensor_copy(xq_w[:], x_w[:].indirect(offs_l[:]))
 
         y_ps = [psum.tile([P, S], F32, name=f"y_ps{t}", tag=f"bank{t}") for t in range(PACK)]
@@ -100,25 +101,30 @@ def tile_picked_ccmpsoftbnorm2_none_po_kernel(
             )
 
         pair_w_raw = sb.tile([P, 2, S], U32, name="pair_w_raw", align_bytes=64)
-        pair_sc_raw = sb.tile([P, 2, S], U8, name="pair_sc_raw", tag="w_sc_raw", align_bytes=64)
+        pair_sc_raw = sb.tile([P, 2, S], U8, name="pair_sc_raw", tag="xq_sc", align_bytes=64)
         pair_w = sb.tile([P, 2, S], U32, name="pair_w", align_bytes=64)
         pair_sc = sb.tile([P, 2, S], U8, name="pair_sc", align_bytes=64)
         for side, offsets in enumerate((cb_l, ca_l)):
-            nc.vector.tensor_copy(pair_sc_raw[:, side, :], x_sc[:].indirect(offsets[:]))
-        for side, offsets in enumerate((cb_l, ca_l)):
             nc.vector.tensor_copy(pair_w_raw[:, side, :], x_w[:].indirect(offsets[:]))
 
-        y_sb = [sb.tile([P, S], F32, name=f"y_sb{t}") for t in range(PACK)]
+        y_sb = [sb.tile([P, S], F32, name=f"y_sb{t}", tag=("xq_w", "w_codes", "y_sb2", "y_sb3")[t], align_bytes=64) for t in range(PACK)]
         y_n2 = [sb.tile([P, S], F32, name=f"y_n2{t}") for t in range(PACK)]
         den = [sb.tile([P, S], F32, name=f"den{t}", tag=f"den{t}") for t in range(PACK)]
         root = [sb.tile([P, S], F32, name=f"root{t}") for t in range(PACK)]
         factor = sb.tile([P, PACK, S], F32, name="factor")
-        for t in range(PACK):
+        for t in (0, 1):
             nc.scalar.activation(y_abs[t][:, :S], y_ps[t][:], ACT.Abs)
-            nc.scalar.activation(y_n2[t][:], y_abs[t][:].indirect(n2_l[:]), ACT.Copy)
-        for t in range(PACK):
-            nc.gpsimd.tensor_tensor(den[t][:], y_abs[t][:, :S], y_n2[t][:], ALU.add)
+        for t in (2, 3):
             nc.vector.tensor_copy(y_sb[t][:], y_ps[t][:])
+        for t in (2, 3):
+            nc.vector.scalar_tensor_tensor(y_abs[t][:, :S], y_ps[t][:], -1.0, y_sb[t][:], ALU.mult, ALU.max)
+        for side, offsets in enumerate((cb_l, ca_l)):
+            nc.vector.tensor_copy(pair_sc_raw[:, side, :], x_sc[:].indirect(offsets[:]))
+        for t in (0, 1):
+            nc.vector.tensor_copy(y_sb[t][:], y_ps[t][:])
+        for t in range(PACK):
+            nc.scalar.activation(y_n2[t][:], y_abs[t][:].indirect(n2_l[:]), ACT.Copy)
+            nc.gpsimd.tensor_tensor(den[t][:], y_abs[t][:, :S], y_n2[t][:], ALU.add)
         for t in range(PACK):
             nc.scalar.activation(root[t][:], den[t][:], ACT.Abs_reciprocal_sqrt, bias=0.5)
         for t in range(PACK):
@@ -146,7 +152,7 @@ def tile_picked_ccmpsoftbnorm2_none_po_kernel(
             w = c1 - c0
             y_n1 = y_n1_of[c0]
             b_ps = [b_banks[2 * n + t // 2][:, t % 2, :] for t in range(PACK)]
-            z_bf = sb.tile([P, w * PACK], BF16, name=f"z_bf{c0}", align_bytes=64)
+            z_bf = sb.tile([P, w * PACK], BF16, name=f"z_bf{c0}", tag="z_bf", align_bytes=64)
             nc.vector.tensor_tensor(
                 z_bf[:].rearrange("p (c i t) -> p c t i", i=RUN, t=PACK),
                 y_n1[:].rearrange("p t (c i) -> p c t i", i=RUN),
@@ -183,15 +189,15 @@ def tile_picked_ccmpsoftbnorm2_none_po_kernel(
         out_rows = out_0.rearrange("(p t) j -> p t j", t=PACK)
         out_words = out_1[0].rearrange("p n t -> p (n t)").bitcast(I32)
         o_sc = sb.tile([P, S], U8, name="o_sc", align_bytes=64)
-        for (c0, c1), freed in zip(OUT_CHUNKS, ("b_sb2", "b_sb3", "b_n43")):
+        for n, (c0, c1) in enumerate(OUT_CHUNKS):
             w = c1 - c0
-            a_n3 = sb.tile([P, PACK, w], F32, name=f"a_n3_{c0}", tag=freed)
+            a_n3 = sb.tile([P, PACK, w], F32, name=f"a_n3_{c0}", tag=("b_sb2", "b_sb3", "b_n43")[n])
             for t in range(PACK):
                 nc.scalar.activation(a_n3[:, t, :], a_sb[t][:].indirect(list_slice(n3_l, c0, c1)), ACT.Copy)
-            res = sb.tile([P, PACK, w], F32, name=f"res{c0}")
+            res = sb.tile([P, PACK, w], F32, name=f"res{c0}", tag=("res0", "res1", "o_bf0")[n], align_bytes=64)
             nc.vector.tensor_tensor(res[:], a_n3[:], prod[:, :, c0:c1], ALU.subtract)
             nc.sync.dma_start(out_rows[:, :, c0:c1], res[:])
-            o_bf = sb.tile([P, w * PACK], BF16, name=f"o_bf{c0}", align_bytes=64)
+            o_bf = sb.tile([P, w * PACK], BF16, name=f"o_bf{c0}", tag=f"o_bf{n}", align_bytes=64)
             nc.vector.tensor_copy(
                 o_bf[:].rearrange("p (c i t) -> p c t i", i=RUN, t=PACK),
                 res[:].rearrange("p t (c i) -> p c t i", i=RUN),

@@ -21,7 +21,8 @@ PER_COL = 16
 SPARE = 32
 RUN = 4
 Z_CHUNKS = ((0, 256), (256, 512))
-OUT_CHUNKS = ((0, 256), (256, 384), (384, 512))
+OUT_CHUNKS = ((0, 128), (128, 256), (256, 384), (384, 512))
+HALVES = ((0, 256), (256, 512))
 SIXTEENTH = 0.0625
 
 FLOPS = 3 * 2 * 512 * 512 * 512
@@ -85,65 +86,100 @@ def tile_picked_ccmpsoftbnorm2_none_po_kernel(
             w_sc[:].rearrange("p (t m) -> p t m", t=PACK),
             w_sc_raw[:].rearrange("p (m t) -> p t m", t=PACK),
         )
-        xq_w = sb.tile([P, S], U32, name="xq_w", tag="xq_w", align_bytes=64)
-        nc.vector.tensor_copy(xq_w[:], x_w[:].indirect(offs_l[:]))
+        xq_w = {}
+        for (c0, c1), tag in zip(HALVES, ("xq_w", "w_sc_raw")):
+            xq_w[c0] = sb.tile([P, c1 - c0], U32, name=f"xq_w{c0}", tag=tag, align_bytes=64)
+            nc.vector.tensor_copy(xq_w[c0][:], x_w[:].indirect(list_slice(offs_l, c0, c1)))
 
         y_ps = [psum.tile([P, S], F32, name=f"y_ps{t}", tag=f"bank{t}") for t in range(PACK)]
-        for t in range(PACK):
+        y0_late = psum.tile([P, S], F32, name="y0_late", tag="bank7")
+        y_parts = [(0, y_ps[0][:, 0:256], 0, 256), (0, y0_late[:, 256:512], 256, 512)]
+        y_parts = y_parts + [(t, y_ps[t][:], 0, S) for t in range(1, PACK)]
+        y_halves = y_parts[:2] + [(t, y_ps[t][:, c0:c1], c0, c1) for t in range(1, PACK) for c0, c1 in HALVES]
+        for t, sums, c0, c1 in y_halves:
             nc.tensor.matmul_mx(
-                y_ps[t][:],
+                sums,
                 lhsT=w_codes[:, 2 * P * t : 2 * P * (t + 1)].bitcast(FP4X4),
                 lhsT_scale=w_sc[:, P * t : P * (t + 1)],
-                rhs=xq_w[:].bitcast(FP8X4),
-                rhs_scale=xq_sc[:],
+                rhs=xq_w[c0][:].bitcast(FP8X4),
+                rhs_scale=xq_sc[:, c0:c1],
                 start=True,
                 stop=True,
             )
 
-        pair_w_raw = sb.tile([P, 2, S], U32, name="pair_w_raw", align_bytes=64)
-        pair_sc_raw = sb.tile([P, 2, S], U8, name="pair_sc_raw", tag="xq_sc", align_bytes=64)
         pair_w = sb.tile([P, 2, S], U32, name="pair_w", align_bytes=64)
         pair_sc = sb.tile([P, 2, S], U8, name="pair_sc", align_bytes=64)
-        for side, offsets in enumerate((cb_l, ca_l)):
-            nc.vector.tensor_copy(pair_w_raw[:, side, :], x_w[:].indirect(offsets[:]))
+
+        def pick_words(side, offsets, tag):
+            raw = sb.tile([P, S], U32, name=f"pair_w_raw{side}", tag=tag, align_bytes=64)
+            nc.vector.tensor_copy(raw[:], x_w[:].indirect(offsets[:]))
+            return raw
+
+        def pick_scales(side, offsets, tag):
+            raw = sb.tile([P, S], U8, name=f"pair_sc_raw{side}", tag=tag, align_bytes=64)
+            nc.vector.tensor_copy(raw[:], x_sc[:].indirect(offsets[:]))
+            return raw
+
+        def deal(dst, src, run):
+            nc.vector.tensor_copy(
+                dst.rearrange("p (t c i) -> p c t i", t=PACK, i=run),
+                src.rearrange("p (c i t) -> p c t i", t=PACK, i=run),
+            )
+
+        cb_words = pick_words(0, cb_l, "cb_words")
 
         y_sb = [sb.tile([P, S], F32, name=f"y_sb{t}", tag=("xq_w", "w_codes", "y_sb2", "y_sb3")[t], align_bytes=64) for t in range(PACK)]
-        y_n2 = [sb.tile([P, S], F32, name=f"y_n2{t}") for t in range(PACK)]
+        y_n2 = [sb.tile([P, S], F32, name=f"y_n2{t}", tag=f"y_n2{t}", align_bytes=64) for t in range(PACK)]
         den = [sb.tile([P, S], F32, name=f"den{t}", tag=f"den{t}") for t in range(PACK)]
-        root = [sb.tile([P, S], F32, name=f"root{t}") for t in range(PACK)]
+        b_sb = [sb.tile([P, 2 * S], F32, name=f"b_sb{t}", tag=f"b_sb{t}") for t in range(PACK)]
+        root = [b_sb[t][:, S:] for t in range(PACK)]
         factor = sb.tile([P, PACK, S], F32, name="factor")
-        for t in (0, 1):
-            nc.scalar.activation(y_abs[t][:, :S], y_ps[t][:], ACT.Abs)
+        for t, sums, c0, c1 in y_parts[:3]:
+            nc.scalar.activation(y_abs[t][:, c0:c1], sums, ACT.Abs)
         for t in (2, 3):
             nc.vector.tensor_copy(y_sb[t][:], y_ps[t][:])
         for t in (2, 3):
             nc.vector.scalar_tensor_tensor(y_abs[t][:, :S], y_ps[t][:], -1.0, y_sb[t][:], ALU.mult, ALU.max)
-        for side, offsets in enumerate((cb_l, ca_l)):
-            nc.vector.tensor_copy(pair_sc_raw[:, side, :], x_sc[:].indirect(offsets[:]))
-        for t in (0, 1):
-            nc.vector.tensor_copy(y_sb[t][:], y_ps[t][:])
+        for t, sums, c0, c1 in y_parts[:3]:
+            nc.vector.tensor_copy(y_sb[t][:, c0:c1], sums)
         for t in range(PACK):
             nc.scalar.activation(y_n2[t][:], y_abs[t][:].indirect(n2_l[:]), ACT.Copy)
             nc.gpsimd.tensor_tensor(den[t][:], y_abs[t][:, :S], y_n2[t][:], ALU.add)
+        ca_words = pick_words(1, ca_l, "y_n20")
+        cb_scales = pick_scales(0, cb_l, "y_n21")
+        ca_scales = pick_scales(1, ca_l, "y_n22")
         for t in range(PACK):
-            nc.scalar.activation(root[t][:], den[t][:], ACT.Abs_reciprocal_sqrt, bias=0.5)
+            nc.scalar.activation(root[t], den[t][:], ACT.Abs_reciprocal_sqrt, bias=0.5)
         for t in range(PACK):
-            nc.vector.scalar_tensor_tensor(factor[:, t, :], root[t][:], gs_sb[:, t : t + 1], root[t][:], ALU.mult, ALU.mult)
+            nc.vector.scalar_tensor_tensor(factor[:, t, :], root[t], gs_sb[:, t : t + 1], root[t], ALU.mult, ALU.mult)
 
-        nc.vector.tensor_copy(
-            pair_w[:].bitcast(I32).rearrange("p s (t m) -> p s t m", t=PACK),
-            pair_w_raw[:].bitcast(I32).rearrange("p s (m t) -> p s t m", t=PACK),
-        )
-        nc.vector.tensor_copy(
-            pair_sc[:].rearrange("p s (t m) -> p s t m", t=PACK),
-            pair_sc_raw[:].rearrange("p s (m t) -> p s t m", t=PACK),
-        )
+        deal(pair_w[:, 0, :].bitcast(I32), cb_words[:].bitcast(I32), 4)
+        deal(pair_sc[:, 0, :], cb_scales[:], 16)
+        deal(pair_w[:, 1, :].bitcast(I32), ca_words[:].bitcast(I32), 4)
+        deal(pair_sc[:, 1, :], ca_scales[:], 16)
 
         b_banks = [psum.tile([P, 2, S // 2], F32, name=f"b_bank{n}", tag=f"bank{PACK + n}") for n in range(PACK)]
-        a_ps = [psum.tile([P, S], F32, name=f"a_ps{t}", tag=f"bank{t}") for t in range(PACK)]
-        b_sb = [sb.tile([P, 2 * S], F32, name=f"b_sb{t}", tag=f"b_sb{t}") for t in range(PACK)]
-        a_sb = [sb.tile([P, S], F32, name=f"a_sb{t}") for t in range(PACK)]
+        b_tanh = sb.tile([P, PACK, S], F32, name="b_tanh")
+
+        def interleave(dst, src):
+            nc.vector.tensor_copy(
+                dst[:].rearrange("p (c i t) -> p c t i", i=RUN, t=PACK),
+                src[:].rearrange("p t (c i) -> p c t i", i=RUN),
+            )
+
+        def score(sums, side, t, z_chunk):
+            nc.tensor.matmul_mx(
+                sums,
+                lhsT=pair_w[:, side, P * t : P * (t + 1)].bitcast(FP8X4),
+                lhsT_scale=pair_sc[:, side, P * t : P * (t + 1)],
+                rhs=z_chunk[0][:].bitcast(FP8X4),
+                rhs_scale=z_chunk[1][:],
+                start=True,
+                stop=True,
+            )
+
         y_n1_of = {}
+        z_of = {}
         for n, (c0, c1) in enumerate(Z_CHUNKS):
             y_n1_of[c0] = sb.tile([P, PACK, c1 - c0], F32, name=f"y_n1_{c0}", tag=f"den{PACK - 1 - n}")
             for t in range(PACK):
@@ -152,56 +188,49 @@ def tile_picked_ccmpsoftbnorm2_none_po_kernel(
             w = c1 - c0
             y_n1 = y_n1_of[c0]
             b_ps = [b_banks[2 * n + t // 2][:, t % 2, :] for t in range(PACK)]
+            z_rows = sb.tile([P, PACK, w], BF16, name=f"z_rows{c0}")
+            for t in range(PACK):
+                nc.vector.tensor_tensor(z_rows[:, t, :], y_n1[:, t, :], factor[:, t, c0:c1], ALU.mult)
             z_bf = sb.tile([P, w * PACK], BF16, name=f"z_bf{c0}", tag="z_bf", align_bytes=64)
-            nc.vector.tensor_tensor(
-                z_bf[:].rearrange("p (c i t) -> p c t i", i=RUN, t=PACK),
-                y_n1[:].rearrange("p t (c i) -> p c t i", i=RUN),
-                factor[:, :, c0:c1].rearrange("p t (c i) -> p c t i", i=RUN),
-                ALU.mult,
-            )
+            interleave(z_bf, z_rows)
             z_w = sb.tile([P, w], U32, name=f"z_w{c0}", align_bytes=64)
             z_sc = sb.tile([P, w], U8, name=f"z_sc{c0}", align_bytes=64)
             nc.vector.quantize_mx(z_w[:].bitcast(FP8X4), z_sc[:], z_bf[:])
-            for side, sums in enumerate((b_ps, [bank[:, c0:c1] for bank in a_ps])):
-                for t in range(PACK):
-                    nc.tensor.matmul_mx(
-                        sums[t],
-                        lhsT=pair_w[:, side, P * t : P * (t + 1)].bitcast(FP8X4),
-                        lhsT_scale=pair_sc[:, side, P * t : P * (t + 1)],
-                        rhs=z_w[:].bitcast(FP8X4),
-                        rhs_scale=z_sc[:],
-                        start=True,
-                        stop=True,
-                    )
+            z_of[c0] = (z_w, z_sc)
             for t in range(PACK):
-                nc.scalar.activation(b_sb[t][:, S + c0 : S + c1], b_ps[t], ACT.Tanh, scale=SIXTEENTH)
+                score(b_ps[t], 0, t, z_of[c0])
+            for h in range(2):
+                nc.scalar.activation(b_tanh[:, 2 * h : 2 * h + 2, c0:c1], b_banks[2 * n + h][:], ACT.Tanh, scale=SIXTEENTH)
             for t in range(PACK):
                 nc.vector.tensor_scalar(b_sb[t][:, c0:c1], b_ps[t], SIXTEENTH, None, ALU.mult)
 
-        b_n4 = [sb.tile([P, S], F32, name=f"b_n4{t}", tag=f"b_n4{t}") for t in range(PACK)]
+        a_ps = [psum.tile([P, S], F32, name=f"a_ps{t}", tag=f"bank{(0, 1, 2, 7)[t]}") for t in range(PACK)]
+        for t in range(PACK):
+            for c0, c1 in Z_CHUNKS:
+                score(a_ps[t][:, c0:c1], 1, t, z_of[c0])
+
+        b_n4 = [sb.tile([P, S], F32, name=f"b_n4{t}", tag=f"b_n4{t}", align_bytes=64) for t in range(PACK)]
         prod = sb.tile([P, PACK, S], F32, name="prod")
         for t in range(PACK):
             nc.scalar.activation(b_n4[t][:], b_sb[t][:].indirect(n4_l[:]), ACT.Copy)
+        a_sb = [sb.tile([P, S], F32, name=f"a_sb{t}", tag=("b_sb0", "b_sb1", "b_sb2", "a_sb3")[t]) for t in range(PACK)]
         for t in range(PACK):
+            nc.vector.tensor_tensor(prod[:, t, :], b_tanh[:, t, :], b_n4[t][:], ALU.mult)
             nc.vector.tensor_scalar(a_sb[t][:], a_ps[t][:], SIXTEENTH, None, ALU.mult)
-            nc.vector.tensor_tensor(prod[:, t, :], b_sb[t][:, S:], b_n4[t][:], ALU.mult)
 
         out_rows = out_0.rearrange("(p t) j -> p t j", t=PACK)
         out_words = out_1[0].rearrange("p n t -> p (n t)").bitcast(I32)
         o_sc = sb.tile([P, S], U8, name="o_sc", align_bytes=64)
         for n, (c0, c1) in enumerate(OUT_CHUNKS):
             w = c1 - c0
-            a_n3 = sb.tile([P, PACK, w], F32, name=f"a_n3_{c0}", tag=("b_sb2", "b_sb3", "b_n43")[n])
+            a_n3 = sb.tile([P, PACK, w], F32, name=f"a_n3_{c0}", tag=f"b_n4{2 + n % 2}", align_bytes=64)
             for t in range(PACK):
                 nc.scalar.activation(a_n3[:, t, :], a_sb[t][:].indirect(list_slice(n3_l, c0, c1)), ACT.Copy)
-            res = sb.tile([P, PACK, w], F32, name=f"res{c0}", tag=("res0", "res1", "o_bf0")[n], align_bytes=64)
+            res = sb.tile([P, PACK, w], F32, name=f"res{c0}", tag=f"res{n}" if n < 2 else f"o_bf{n - 2}", align_bytes=64)
             nc.vector.tensor_tensor(res[:], a_n3[:], prod[:, :, c0:c1], ALU.subtract)
             nc.sync.dma_start(out_rows[:, :, c0:c1], res[:])
             o_bf = sb.tile([P, w * PACK], BF16, name=f"o_bf{c0}", tag=f"o_bf{n}", align_bytes=64)
-            nc.vector.tensor_copy(
-                o_bf[:].rearrange("p (c i t) -> p c t i", i=RUN, t=PACK),
-                res[:].rearrange("p t (c i) -> p c t i", i=RUN),
-            )
+            interleave(o_bf, res)
             o_w = sb.tile([P, w], U32, name=f"o_w{c0}", align_bytes=64)
             nc.vector.quantize_mx(o_w[:].bitcast(FP8X4), o_sc[:, c0:c1], o_bf[:])
             nc.sync.dma_start(out_words[:, c0:c1], o_w[:].bitcast(I32))

from contextlib import ExitStack

import concourse.mybir as mybir

F32 = mybir.dt.float32
BF16 = mybir.dt.bfloat16
I32 = mybir.dt.int32
U32 = mybir.dt.uint32
U16 = mybir.dt.uint16
U8 = mybir.dt.uint8
FP8X4 = mybir.dt.float8_e4m3fn_x4
FP4X4 = mybir.dt.float4_e2m1fn_x4
ACT = mybir.ActivationFunctionType
ALU = mybir.AluOpType

P = 128
PACK = 4
T = 2048
S = 512
PER_COL = 16
SPARE = 32
RUN = 4
Z_CHUNKS = ((0, 256), (256, 512))
OUT_CHUNKS = ((0, 128), (128, 256), (256, 384), (384, 512))
HALVES = ((0, 256), (256, 512))
SIXTEENTH = 0.0625

FLOPS = 3 * 2 * 512 * 512 * 512


def list_slice(offsets, c0, c1):
    return offsets[:, c0 // PER_COL : c1 // PER_COL]


def tile_picked_ccmpsoftbnorm2_none_po_kernel(
    tc, x_words, x_scales, w1_words, w1_scales, gs, offs, n1, n2, ca, cb, n3, n4, out_0, out_1, out_2
):
    nc = tc.nc
    with ExitStack() as ctx:
        lists = ctx.enter_context(tc.tile_pool(name="lists", bufs=1))
        sb = ctx.enter_context(tc.tile_pool(name="sb", bufs=1))
        psum = ctx.enter_context(tc.psum_pool(name="psum", bufs=1))

        def load_list(name, src):
            tile = lists.tile([P, S // PER_COL], U16, name=name)
            nc.sync.dma_start(tile[:], src)
            return tile

        x_sc = sb.tile([P, T], U8, name="x_sc", align_bytes=64)
        w_sc_raw = sb.tile([P, S], U8, name="w_sc_raw", tag="w_sc_raw", align_bytes=64)
        nc.gpsimd.memset(x_sc[:].bitcast(I32), 0)
        nc.gpsimd.memset(w_sc_raw[:].bitcast(I32), 0)
        x_w = sb.tile([P, T], U32, name="x_w", align_bytes=64)
        w_raw = sb.tile([P, 2 * S], U8, name="w_raw", align_bytes=64)
        offs_l = load_list("offs_l", offs)
        nc.sync.dma_start(w_raw[:].bitcast(I32), w1_words[0].bitcast(I32))
        for q in range(4):
            nc.sync.dma_start(x_sc[32 * q : 32 * q + 4, :].bitcast(I32), x_scales[0, 4 * q : 4 * q + 4, :].bitcast(I32))
        nc.sync.dma_start(x_w[:].bitcast(I32), x_words[0].rearrange("p n t -> p (n t)").bitcast(I32))
        for q in range(4):
            nc.sync.dma_start(w_sc_raw[32 * q : 32 * q + 4, :].bitcast(I32), w1_scales[0, 4 * q : 4 * q + 4, :].bitcast(I32))
        cb_l = load_list("cb_l", cb)
        ca_l = load_list("ca_l", ca)
        n2_l = load_list("n2_l", n2)
        gs_sb = sb.tile([P, PACK], F32, name="gs_sb")
        nc.sync.dma_start(gs_sb[:], gs.rearrange("(p t) o -> p (t o)", t=PACK))
        n1_l = load_list("n1_l", n1)
        n4_l = load_list("n4_l", n4)
        n3_l = load_list("n3_l", n3)

        y_abs = [sb.tile([P, S + SPARE], F32, name=f"y_abs{t}") for t in range(PACK)]
        for t in range(PACK):
            nc.vector.memset(y_abs[t][:, S:], 0.0)
        warm = sb.tile([P, 1], F32, name="warm")
        nc.scalar.activation(warm[:], y_abs[0][:, S : S + 1], ACT.Abs_reciprocal_sqrt, bias=0.5)

        w_codes = sb.tile([P, 2 * S], U8, name="w_codes", tag="w_codes", align_bytes=64)
        nc.vector.tensor_copy(
            w_codes[:].rearrange("p (t m b) -> p t m b", t=PACK, b=2),
            w_raw[:].rearrange("p (m t b) -> p t m b", t=PACK, b=2),
        )
        xq_sc = sb.tile([P, S], U8, name="xq_sc", tag="xq_sc", align_bytes=64)
        nc.vector.tensor_copy(xq_sc[:], x_sc[:].indirect(offs_l[:]))
        w_sc = sb.tile([P, S], U8, name="w_sc", align_bytes=64)
        nc.vector.tensor_copy(
            w_sc[:].rearrange("p (t m) -> p t m", t=PACK),
            w_sc_raw[:].rearrange("p (m t) -> p t m", t=PACK),
        )
        xq_w = {}
        for (c0, c1), tag in zip(HALVES, ("xq_w", "w_sc_raw")):
            xq_w[c0] = sb.tile([P, c1 - c0], U32, name=f"xq_w{c0}", tag=tag, align_bytes=64)
            nc.vector.tensor_copy(xq_w[c0][:], x_w[:].indirect(list_slice(offs_l, c0, c1)))

        y_ps = [psum.tile([P, S], F32, name=f"y_ps{t}", tag=f"bank{t}") for t in range(PACK)]
        y0_late = psum.tile([P, S], F32, name="y0_late", tag="bank7")
        y_parts = [(0, y_ps[0][:, 0:256], 0, 256), (0, y0_late[:, 256:512], 256, 512)]
        y_parts = y_parts + [(t, y_ps[t][:], 0, S) for t in range(1, PACK)]
        y_halves = y_parts[:2] + [(t, y_ps[t][:, c0:c1], c0, c1) for t in range(1, PACK) for c0, c1 in HALVES]
        for t, sums, c0, c1 in y_halves:
            nc.tensor.matmul_mx(
                sums,
                lhsT=w_codes[:, 2 * P * t : 2 * P * (t + 1)].bitcast(FP4X4),
                lhsT_scale=w_sc[:, P * t : P * (t + 1)],
                rhs=xq_w[c0][:].bitcast(FP8X4),
                rhs_scale=xq_sc[:, c0:c1],
                start=True,
                stop=True,
            )

        pair_w = sb.tile([P, 2, S], U32, name="pair_w", align_bytes=64)
        pair_sc = sb.tile([P, 2, S], U8, name="pair_sc", align_bytes=64)

        def pick_words(side, offsets, tag):
            raw = sb.tile([P, S], U32, name=f"pair_w_raw{side}", tag=tag, align_bytes=64)
            nc.vector.tensor_copy(raw[:], x_w[:].indirect(offsets[:]))
            return raw

        def pick_scales(side, offsets, tag):
            raw = sb.tile([P, S], U8, name=f"pair_sc_raw{side}", tag=tag, align_bytes=64)
            nc.vector.tensor_copy(raw[:], x_sc[:].indirect(offsets[:]))
            return raw

        def deal(dst, src, run):
            nc.vector.tensor_copy(
                dst.rearrange("p (t c i) -> p c t i", t=PACK, i=run),
                src.rearrange("p (c i t) -> p c t i", t=PACK, i=run),
            )

        cb_words = pick_words(0, cb_l, "cb_words")

        y_sb = [sb.tile([P, S], F32, name=f"y_sb{t}", tag=("xq_w", "w_codes", "y_sb2", "y_sb3")[t], align_bytes=64) for t in range(PACK)]
        y_n2 = [sb.tile([P, S], F32, name=f"y_n2{t}", tag=f"y_n2{t}", align_bytes=64) for t in range(PACK)]
        den = [sb.tile([P, S], F32, name=f"den{t}", tag=f"den{t}") for t in range(PACK)]
        b_sb = [sb.tile([P, 2 * S], F32, name=f"b_sb{t}", tag=f"b_sb{t}") for t in range(PACK)]
        root = [b_sb[t][:, S:] for t in range(PACK)]
        factor = sb.tile([P, PACK, S], F32, name="factor")
        for t, sums, c0, c1 in y_parts[:3]:
            nc.scalar.activation(y_abs[t][:, c0:c1], sums, ACT.Abs)
        for t in (2, 3):
            nc.vector.tensor_copy(y_sb[t][:], y_ps[t][:])
        for t in (2, 3):
            nc.vector.scalar_tensor_tensor(y_abs[t][:, :S], y_ps[t][:], -1.0, y_sb[t][:], ALU.mult, ALU.max)
        for t, sums, c0, c1 in y_parts[:3]:
            nc.vector.tensor_copy(y_sb[t][:, c0:c1], sums)
        for t in range(PACK):
            nc.scalar.activation(y_n2[t][:], y_abs[t][:].indirect(n2_l[:]), ACT.Copy)
            nc.gpsimd.tensor_tensor(den[t][:], y_abs[t][:, :S], y_n2[t][:], ALU.add)
        ca_words = pick_words(1, ca_l, "y_n20")
        cb_scales = pick_scales(0, cb_l, "y_n21")
        ca_scales = pick_scales(1, ca_l, "y_n22")
        for t in range(PACK):
            nc.scalar.activation(root[t], den[t][:], ACT.Abs_reciprocal_sqrt, bias=0.5)
        for t in range(PACK):
            nc.vector.scalar_tensor_tensor(factor[:, t, :], root[t], gs_sb[:, t : t + 1], root[t], ALU.mult, ALU.mult)

        deal(pair_w[:, 0, :].bitcast(I32), cb_words[:].bitcast(I32), 4)
        deal(pair_sc[:, 0, :], cb_scales[:], 16)
        deal(pair_w[:, 1, :].bitcast(I32), ca_words[:].bitcast(I32), 4)
        deal(pair_sc[:, 1, :], ca_scales[:], 16)

        b_banks = [psum.tile([P, 2, S // 2], F32, name=f"b_bank{n}", tag=f"bank{PACK + n}") for n in range(PACK)]
        b_tanh = sb.tile([P, PACK, S], F32, name="b_tanh")

        def interleave(dst, src):
            nc.vector.tensor_copy(
                dst[:].rearrange("p (c i t) -> p c t i", i=RUN, t=PACK),
                src[:].rearrange("p t (c i) -> p c t i", i=RUN),
            )

        def score(sums, side, t, z_chunk):
            nc.tensor.matmul_mx(
                sums,
                lhsT=pair_w[:, side, P * t : P * (t + 1)].bitcast(FP8X4),
                lhsT_scale=pair_sc[:, side, P * t : P * (t + 1)],
                rhs=z_chunk[0][:].bitcast(FP8X4),
                rhs_scale=z_chunk[1][:],
                start=True,
                stop=True,
            )

        y_n1_of = {}
        z_of = {}
        for n, (c0, c1) in enumerate(Z_CHUNKS):
            y_n1_of[c0] = sb.tile([P, PACK, c1 - c0], F32, name=f"y_n1_{c0}", tag=f"den{PACK - 1 - n}")
            for t in range(PACK):
                nc.scalar.activation(y_n1_of[c0][:, t, :], y_sb[t][:].indirect(list_slice(n1_l, c0, c1)), ACT.Copy)
        for n, (c0, c1) in enumerate(Z_CHUNKS):
            w = c1 - c0
            y_n1 = y_n1_of[c0]
            b_ps = [b_banks[2 * n + t // 2][:, t % 2, :] for t in range(PACK)]
            z_rows = sb.tile([P, PACK, w], BF16, name=f"z_rows{c0}")
            for t in range(PACK):
                nc.vector.tensor_tensor(z_rows[:, t, :], y_n1[:, t, :], factor[:, t, c0:c1], ALU.mult)
            z_bf = sb.tile([P, w * PACK], BF16, name=f"z_bf{c0}", tag="z_bf", align_bytes=64)
            interleave(z_bf, z_rows)
            z_w = sb.tile([P, w], U32, name=f"z_w{c0}", align_bytes=64)
            z_sc = sb.tile([P, w], U8, name=f"z_sc{c0}", align_bytes=64)
            nc.vector.quantize_mx(z_w[:].bitcast(FP8X4), z_sc[:], z_bf[:])
            z_of[c0] = (z_w, z_sc)
            for t in range(PACK):
                score(b_ps[t], 0, t, z_of[c0])
            for h in range(2):
                nc.scalar.activation(b_tanh[:, 2 * h : 2 * h + 2, c0:c1], b_banks[2 * n + h][:], ACT.Tanh, scale=SIXTEENTH)
            for t in range(PACK):
                nc.vector.tensor_scalar(b_sb[t][:, c0:c1], b_ps[t], SIXTEENTH, None, ALU.mult)

        a_ps = [psum.tile([P, S], F32, name=f"a_ps{t}", tag=f"bank{(0, 1, 2, 7)[t]}") for t in range(PACK)]
        for t in range(PACK):
            for c0, c1 in Z_CHUNKS:
                score(a_ps[t][:, c0:c1], 1, t, z_of[c0])

        b_n4 = [sb.tile([P, S], F32, name=f"b_n4{t}", tag=f"b_n4{t}", align_bytes=64) for t in range(PACK)]
        prod = sb.tile([P, PACK, S], F32, name="prod")
        for t in range(PACK):
            nc.scalar.activation(b_n4[t][:], b_sb[t][:].indirect(n4_l[:]), ACT.Copy)
        a_sb = [sb.tile([P, S], F32, name=f"a_sb{t}", tag=("b_sb0", "b_sb1", "b_sb2", "a_sb3")[t]) for t in range(PACK)]
        for t in range(PACK):
            nc.vector.tensor_tensor(prod[:, t, :], b_tanh[:, t, :], b_n4[t][:], ALU.mult)
            nc.vector.tensor_scalar(a_sb[t][:], a_ps[t][:], SIXTEENTH, None, ALU.mult)

        out_rows = out_0.rearrange("(p t) j -> p t j", t=PACK)
        out_words = out_1[0].rearrange("p n t -> p (n t)").bitcast(I32)
        o_sc = sb.tile([P, S], U8, name="o_sc", align_bytes=64)
        for n, (c0, c1) in enumerate(OUT_CHUNKS):
            w = c1 - c0
            a_n3 = sb.tile([P, PACK, w], F32, name=f"a_n3_{c0}", tag=f"b_n4{2 + n % 2}", align_bytes=64)
            for t in range(PACK):
                nc.scalar.activation(a_n3[:, t, :], a_sb[t][:].indirect(list_slice(n3_l, c0, c1)), ACT.Copy)
            res = sb.tile([P, PACK, w], F32, name=f"res{c0}", tag=f"res{n}" if n < 2 else f"o_bf{n - 2}", align_bytes=64)
            nc.vector.tensor_tensor(res[:], a_n3[:], prod[:, :, c0:c1], ALU.subtract)
            nc.sync.dma_start(out_rows[:, :, c0:c1], res[:])
            o_bf = sb.tile([P, w * PACK], BF16, name=f"o_bf{c0}", tag=f"o_bf{n}", align_bytes=64)
            interleave(o_bf, res)
            o_w = sb.tile([P, w], U32, name=f"o_w{c0}", align_bytes=64)
            nc.vector.quantize_mx(o_w[:].bitcast(FP8X4), o_sc[:, c0:c1], o_bf[:])
            nc.sync.dma_start(out_words[:, c0:c1], o_w[:].bitcast(I32))
        for q in range(4):
            queue = nc.scalar if q % 2 else nc.sync
            queue.dma_start(out_2[0, 4 * q : 4 * q + 4, :].bitcast(I32), o_sc[32 * q : 32 * q + 4, :].bitcast(I32))
